import numpy as np, ml_dtypes
CORES = [3,5,19,21,35,37,51,53,67,69]
N = 10
TK = 256
def gelu(z): return 0.5 * z * (1.0 + np.tanh(0.7978845608028654 * (z + 0.044715 * z ** 3)))
def setup_inputs(rng):
    return {"x": rng.standard_normal((N, 128, TK), dtype=np.float32).astype(ml_dtypes.bfloat16), "w1": (rng.standard_normal((N, 128, 128), dtype=np.float32) / 8).astype(ml_dtypes.bfloat16), "w2": (rng.standard_normal((N, 128, 128), dtype=np.float32) / 8).astype(ml_dtypes.bfloat16)}
def setup_inputs_big(rng):
    d = setup_inputs(rng)
    for k in ("x",): d[k] = (d[k].astype(np.float32) * 1024.0).astype(d[k].dtype)
    return d
def setup_inputs_small(rng):
    d = setup_inputs(rng)
    for k in ("x",): d[k] = (d[k].astype(np.float32) * (1 / 1024.0)).astype(d[k].dtype)
    return d
def setup_inputs_apart(rng):
    d = setup_inputs(rng)
    f = (10.0 ** rng.permutation(np.linspace(-1.5, 1.5, N))).astype(np.float32).reshape(N, 1, 1)
    for k in ("x",): d[k] = (d[k].astype(np.float32) * f).astype(d[k].dtype)
    return d
def reference(x, w1, w2):
    X, W1, W2 = x.astype(np.float64), w1.astype(np.float64), w2.astype(np.float64)
    y = np.zeros((N, 128, TK))
    for r in range(N):
        for j in range(N):
            y[r] += W2[j].T @ (gelu(W1[j].T @ X[r]))
    return {"y": y.astype(ml_dtypes.bfloat16)}

@@ -1,0 +1,139 @@
+from concourse.bass import DstId, RemoteDMATransfer
+from concourse.mybir import ActivationFunctionType
+
+N_SLICES = 10
+TOK = 256
+SW = 256
+N_HB = 7
+
+FORWARD = (1, 2)
+DIRECT = (3, 4)
+
+OWN, SIB = 0, 1
+
+
+def _same(o):
+    return 1 + o
+
+
+def _other(o):
+    return 5 + o
+
+
+ORDER = [OWN, _same(1), SIB, _same(2), _same(3), _other(3), _other(1), _other(2), _same(4), _other(4)]
+
+SCRATCH = {
+    "W": ("sbuf", [128, N_SLICES * SW], "bfloat16"),
+    "X": ("sbuf", [128, TOK], "bfloat16"),
+    "G": ("sbuf", [128, N_SLICES * TOK], "bfloat16"),
+    "Yo": ("sbuf", [128, TOK], "bfloat16"),
+    "yacc": ("psum", [128, 512], "float32"),
+}
+for _k in range(N_HB):
+    SCRATCH["h%d" % _k] = ("psum", [128, 512], "float32")
+
+SEMAPHORES = (["wld", "xld", "yd", "cp", "st", "sent"]
+              + ["a%d" % s for s in range(1, N_SLICES)]
+              + ["hd%d" % k for k in range(N_SLICES)]
+              + ["gd%d" % k for k in range(N_SLICES)])
+
+
+def _bits(mask):
+    return [e for e in range(mask.bit_length()) if (mask >> e) & 1]
+
+
+def _mask(engines):
+    m = 0
+    for e in engines:
+        m |= 1 << e
+    return m
+
+
+def rank_program(g, core, T, topo):
+    if T.rank_of(core) is None:
+        return
+    sem = T.sem
+    W, X, G = T.W, T.X, T.G
+
+    def slot(s):
+        return W[:, s * SW:(s + 1) * SW]
+
+    chips = []
+    for c in T.cores:
+        if topo.chip(c) not in chips:
+            chips.append(topo.chip(c))
+    here = chips.index(topo.chip(core))
+    sib = [c for c in T.cores if topo.chip(c) == topo.chip(core) and c != core][0]
+
+    def far(o, same_die):
+        ch = chips[(here + o) % len(chips)]
+        c = [c for c in T.cores if topo.chip(c) == ch and (topo.die(c) == topo.die(core)) == same_die][0]
+        assert topo.may_write(core, c)
+        return c
+
+    e_off = _bits(topo.mask(core, far(1, True)))
+    e_loc = [e for e in _bits(topo.mask(core, sib)) if e not in e_off]
+    half = len(e_off) // 2
+    n_land = {SIB: len(e_loc)}
+    for o in FORWARD:
+        n_land[_same(o)] = len(e_off)
+        n_land[_other(o)] = len(e_loc)
+    for o in DIRECT:
+        n_land[_same(o)] = half
+        n_land[_other(o)] = len(e_off) - half
+
+    sent = [0]
+
+    def send(dst_core, dst_slot, src_slot, engines):
+        rid, pid, _ = topo.addr(dst_core)
+        sent[0] += len(engines)
+        return RemoteDMATransfer(dst_ids=[DstId(rid=rid, pnc=pid)], dma_engine_mask=_mask(engines),
+                                 remote_sem=sem["a%d" % dst_slot], src=slot(src_slot), dst=slot(dst_slot))
+
+    g.sync.dma_start(W[:, 0:128], T.w1[:, :]).then_inc(sem.wld, 16)
+    g.scalar.dma_start(W[:, 128:256], T.w2[:, :]).then_inc(sem.wld, 16)
+    g.sync.dma_start(X[:, :], T.x[:, :]).then_inc(sem.xld, 16)
+
+    g.wait_ge(sem.wld, 32)
+    for o in FORWARD:
+        g.remote_dma_fused([send(far(o, True), _same(o), OWN, e_off)], local_sem=sem.sent)
+    for o in DIRECT:
+        g.remote_dma_fused([send(far(o, True), _same(o), OWN, e_off[:half]),
+                            send(far(o, False), _other(o), OWN, e_off[half:])], local_sem=sem.sent)
+    g.remote_dma_fused([send(sib, SIB, OWN, e_loc)], local_sem=sem.sent)
+    for o in FORWARD:
+        g.wait_ge(sem["a%d" % _same(o)], n_land[_same(o)])
+        g.remote_dma_fused([send(sib, _other(o), _same(o), e_loc)], local_sem=sem.sent)
+
+    pe = g.tensor
+    n = len(ORDER)
+
+    def second(k):
+        s = ORDER[k]
+        pe.wait_ge(sem["gd%d" % k], 1)
+        pe.matmul(T.yacc[:, 0:TOK], W[:, s * SW + 128:(s + 1) * SW], G[:, k * TOK:(k + 1) * TOK],
+                  k == 0, k == n - 1).then_inc(sem.yd, 1)
+
+    for k, s in enumerate(ORDER):
+        if s == OWN:
+            pe.wait_ge(sem.wld, 32)
+            pe.wait_ge(sem.xld, 16)
+        else:
+            pe.wait_ge(sem["a%d" % s], n_land[s])
+        pe.matmul(T["h%d" % (k % N_HB)][:, 0:TOK], W[:, s * SW:s * SW + 128], X[:, :], True, True).then_inc(sem["hd%d" % k], 1)
+        if k:
+            second(k - 1)
+    second(n - 1)
+
+    for k in range(n):
+        g.scalar.wait_ge(sem["hd%d" % k], 1)
+        g.scalar.activation(G[:, k * TOK:(k + 1) * TOK], T["h%d" % (k % N_HB)][:, 0:TOK],
+                            ActivationFunctionType.Gelu_apprx_tanh).then_inc(sem["gd%d" % k], 1)
+
+    g.vector.wait_ge(sem.yd, n)
+    g.vector.tensor_copy(T.Yo[:, :], T.yacc[:, 0:TOK]).then_inc(sem.cp, 1)
+    g.sync.wait_ge(sem.cp, 1)
+    g.sync.dma_start(T.y[:, :], T.Yo[:, :]).then_inc(sem.st, 16)
+    g.sync.wait_ge(sem.st, 16)
+
+    g.wait_ge(sem.sent, sent[0])

@@ -3,11 +3,12 @@ from concourse.mybir import ActivationFunctionType
 
 N_SLICES = 10
 TOK = 256
+HALF = TOK // 2
 SW = 256
-N_HB = 7
+N_HB = 6
 
-FORWARD = (1, 2)
-DIRECT = (3, 4)
+FORWARD = (1, 2, 3)
+DIRECT = (4,)
 
 OWN, SIB = 0, 1
 
@@ -20,22 +21,25 @@ def _other(o):
     return 5 + o
 
 
-ORDER = [OWN, _same(1), SIB, _same(2), _same(3), _other(3), _other(1), _other(2), _same(4), _other(4)]
+ORDER = [OWN, _same(1), SIB, _same(2), _same(3), _other(1), _same(4), _other(2), _other(4), _other(3)]
+UNITS = [(s, 0, TOK) for s in ORDER[:-1]] + [(ORDER[-1], 0, HALF), (ORDER[-1], HALF, TOK)]
+LOOK = [1] + [2] * (len(UNITS) - 1)
 
 SCRATCH = {
     "W": ("sbuf", [128, N_SLICES * SW], "bfloat16"),
     "X": ("sbuf", [128, TOK], "bfloat16"),
     "G": ("sbuf", [128, N_SLICES * TOK], "bfloat16"),
     "Yo": ("sbuf", [128, TOK], "bfloat16"),
-    "yacc": ("psum", [128, 512], "float32"),
+    "y0": ("psum", [128, 512], "float32"),
+    "y1": ("psum", [128, 512], "float32"),
 }
 for _k in range(N_HB):
     SCRATCH["h%d" % _k] = ("psum", [128, 512], "float32")
 
-SEMAPHORES = (["wld", "xld", "yd", "cp", "st", "sent"]
+SEMAPHORES = (["wld", "xld", "yd0", "yd1", "cp0", "cp1", "st0", "st1", "sent"]
               + ["a%d" % s for s in range(1, N_SLICES)]
-              + ["hd%d" % k for k in range(N_SLICES)]
-              + ["gd%d" % k for k in range(N_SLICES)])
+              + ["hd%d" % u for u in range(len(UNITS))]
+              + ["gd%d" % u for u in range(len(UNITS))])
 
 
 def _bits(mask):
@@ -73,67 +77,86 @@ def rank_program(g, core, T, topo):
 
     e_off = _bits(topo.mask(core, far(1, True)))
     e_loc = [e for e in _bits(topo.mask(core, sib)) if e not in e_off]
-    half = len(e_off) // 2
     n_land = {SIB: len(e_loc)}
     for o in FORWARD:
         n_land[_same(o)] = len(e_off)
         n_land[_other(o)] = len(e_loc)
     for o in DIRECT:
-        n_land[_same(o)] = half
-        n_land[_other(o)] = len(e_off) - half
+        n_land[_same(o)] = len(e_off)
+        n_land[_other(o)] = len(e_off)
 
     sent = [0]
 
-    def send(dst_core, dst_slot, src_slot, engines):
+    def write(dst_core, dst_slot, src_slot, engines):
         rid, pid, _ = topo.addr(dst_core)
         sent[0] += len(engines)
-        return RemoteDMATransfer(dst_ids=[DstId(rid=rid, pnc=pid)], dma_engine_mask=_mask(engines),
-                                 remote_sem=sem["a%d" % dst_slot], src=slot(src_slot), dst=slot(dst_slot))
+        g.remote_dma_fused([RemoteDMATransfer(dst_ids=[DstId(rid=rid, pnc=pid)], dma_engine_mask=_mask(engines),
+                                              remote_sem=sem["a%d" % dst_slot], src=slot(src_slot), dst=slot(dst_slot))],
+                           local_sem=sem.sent)
 
     g.sync.dma_start(W[:, 0:128], T.w1[:, :]).then_inc(sem.wld, 16)
     g.scalar.dma_start(W[:, 128:256], T.w2[:, :]).then_inc(sem.wld, 16)
     g.sync.dma_start(X[:, :], T.x[:, :]).then_inc(sem.xld, 16)
 
     g.wait_ge(sem.wld, 32)
-    for o in FORWARD:
-        g.remote_dma_fused([send(far(o, True), _same(o), OWN, e_off)], local_sem=sem.sent)
+    write(far(FORWARD[0], True), _same(FORWARD[0]), OWN, e_off)
+    write(sib, SIB, OWN, e_loc)
+    for o in FORWARD[1:]:
+        write(far(o, True), _same(o), OWN, e_off)
     for o in DIRECT:
-        g.remote_dma_fused([send(far(o, True), _same(o), OWN, e_off[:half]),
-                            send(far(o, False), _other(o), OWN, e_off[half:])], local_sem=sem.sent)
-    g.remote_dma_fused([send(sib, SIB, OWN, e_loc)], local_sem=sem.sent)
+        write(far(o, True), _same(o), OWN, e_off)
+        write(far(o, False), _other(o), OWN, e_off)
     for o in FORWARD:
         g.wait_ge(sem["a%d" % _same(o)], n_land[_same(o)])
-        g.remote_dma_fused([send(sib, _other(o), _same(o), e_loc)], local_sem=sem.sent)
+        write(sib, _other(o), _same(o), e_loc)
 
     pe = g.tensor
-    n = len(ORDER)
+    n = len(UNITS)
+    tile_of = [min(u, N_SLICES - 1) for u in range(n)]
+    last_of = {0: max(u for u in range(n) if UNITS[u][1] < HALF), 1: max(u for u in range(n) if UNITS[u][2] > HALF)}
+    n_y = {0: 0, 1: 0}
 
-    def second(k):
-        s = ORDER[k]
-        pe.wait_ge(sem["gd%d" % k], 1)
-        pe.matmul(T.yacc[:, 0:TOK], W[:, s * SW + 128:(s + 1) * SW], G[:, k * TOK:(k + 1) * TOK],
-                  k == 0, k == n - 1).then_inc(sem.yd, 1)
+    def first(u):
+        s, c0, c1 = UNITS[u]
+        if u == 0 or UNITS[u - 1][0] != s:
+            if s == OWN:
+                pe.wait_ge(sem.wld, 32)
+                pe.wait_ge(sem.xld, 16)
+            else:
+                pe.wait_ge(sem["a%d" % s], n_land[s])
+        pe.matmul(T["h%d" % (u % N_HB)][:, 0:c1 - c0], W[:, s * SW:s * SW + 128], X[:, c0:c1], True, True).then_inc(sem["hd%d" % u], 1)
 
-    for k, s in enumerate(ORDER):
-        if s == OWN:
-            pe.wait_ge(sem.wld, 32)
-            pe.wait_ge(sem.xld, 16)
-        else:
-            pe.wait_ge(sem["a%d" % s], n_land[s])
-        pe.matmul(T["h%d" % (k % N_HB)][:, 0:TOK], W[:, s * SW:s * SW + 128], X[:, :], True, True).then_inc(sem["hd%d" % k], 1)
-        if k:
-            second(k - 1)
-    second(n - 1)
+    def second(u):
+        s, c0, c1 = UNITS[u]
+        pe.wait_ge(sem["gd%d" % u], 1)
+        for hf in (0, 1):
+            lo, hi = max(c0, hf * HALF), min(c1, (hf + 1) * HALF)
+            if lo >= hi:
+                continue
+            base = tile_of[u] * TOK
+            pe.matmul(T["y%d" % hf][:, 0:HALF], W[:, s * SW + 128:(s + 1) * SW], G[:, base + lo:base + hi],
+                      u == 0, u == last_of[hf]).then_inc(sem["yd%d" % hf], 1)
+            n_y[hf] += 1
 
-    for k in range(n):
-        g.scalar.wait_ge(sem["hd%d" % k], 1)
-        g.scalar.activation(G[:, k * TOK:(k + 1) * TOK], T["h%d" % (k % N_HB)][:, 0:TOK],
-                            ActivationFunctionType.Gelu_apprx_tanh).then_inc(sem["gd%d" % k], 1)
+    pend = 0
+    for u in range(n):
+        first(u)
+        while pend < n and min(pend + LOOK[pend], n - 1) <= u:
+            second(pend)
+            pend += 1
 
-    g.vector.wait_ge(sem.yd, n)
-    g.vector.tensor_copy(T.Yo[:, :], T.yacc[:, 0:TOK]).then_inc(sem.cp, 1)
-    g.sync.wait_ge(sem.cp, 1)
-    g.sync.dma_start(T.y[:, :], T.Yo[:, :]).then_inc(sem.st, 16)
-    g.sync.wait_ge(sem.st, 16)
+    for u in range(n):
+        s, c0, c1 = UNITS[u]
+        base = tile_of[u] * TOK
+        g.scalar.wait_ge(sem["hd%d" % u], 1)
+        g.scalar.activation(G[:, base + c0:base + c1], T["h%d" % (u % N_HB)][:, 0:c1 - c0],
+                            ActivationFunctionType.Gelu_apprx_tanh).then_inc(sem["gd%d" % u], 1)
+
+    for hf, q in ((0, g.sync), (1, g.scalar)):
+        g.vector.wait_ge(sem["yd%d" % hf], n_y[hf])
+        g.vector.tensor_copy(T.Yo[:, hf * HALF:(hf + 1) * HALF], T["y%d" % hf][:, 0:HALF]).then_inc(sem["cp%d" % hf], 1)
+        q.wait_ge(sem["cp%d" % hf], 1)
+        q.dma_start(T.y[:, hf * HALF:(hf + 1) * HALF], T.Yo[:, hf * HALF:(hf + 1) * HALF]).then_inc(sem["st%d" % hf], 16)
+        q.wait_ge(sem["st%d" % hf], 16)
 
     g.wait_ge(sem.sent, sent[0])

from concourse.bass import DstId, RemoteDMATransfer
from concourse.mybir import ActivationFunctionType

N_SLICES = 10
TOK = 256
HALF = TOK // 2
SW = 256
N_HB = 6

FORWARD = (1, 2, 3)
DIRECT = (4,)

OWN, SIB = 0, 1


def _same(o):
    return 1 + o


def _other(o):
    return 5 + o


ORDER = [OWN, _same(1), SIB, _same(2), _same(3), _other(1), _same(4), _other(2), _other(4), _other(3)]
UNITS = [(s, 0, TOK) for s in ORDER[:-1]] + [(ORDER[-1], 0, HALF), (ORDER[-1], HALF, TOK)]
LOOK = [1] + [2] * (len(UNITS) - 1)

SCRATCH = {
    "W": ("sbuf", [128, N_SLICES * SW], "bfloat16"),
    "X": ("sbuf", [128, TOK], "bfloat16"),
    "G": ("sbuf", [128, N_SLICES * TOK], "bfloat16"),
    "Yo": ("sbuf", [128, TOK], "bfloat16"),
    "y0": ("psum", [128, 512], "float32"),
    "y1": ("psum", [128, 512], "float32"),
}
for _k in range(N_HB):
    SCRATCH["h%d" % _k] = ("psum", [128, 512], "float32")

SEMAPHORES = (["wld", "xld", "yd0", "yd1", "cp0", "cp1", "st0", "st1", "sent"]
              + ["a%d" % s for s in range(1, N_SLICES)]
              + ["hd%d" % u for u in range(len(UNITS))]
              + ["gd%d" % u for u in range(len(UNITS))])


def _bits(mask):
    return [e for e in range(mask.bit_length()) if (mask >> e) & 1]


def _mask(engines):
    m = 0
    for e in engines:
        m |= 1 << e
    return m


def rank_program(g, core, T, topo):
    if T.rank_of(core) is None:
        return
    sem = T.sem
    W, X, G = T.W, T.X, T.G

    def slot(s):
        return W[:, s * SW:(s + 1) * SW]

    chips = []
    for c in T.cores:
        if topo.chip(c) not in chips:
            chips.append(topo.chip(c))
    here = chips.index(topo.chip(core))
    sib = [c for c in T.cores if topo.chip(c) == topo.chip(core) and c != core][0]

    def far(o, same_die):
        ch = chips[(here + o) % len(chips)]
        c = [c for c in T.cores if topo.chip(c) == ch and (topo.die(c) == topo.die(core)) == same_die][0]
        assert topo.may_write(core, c)
        return c

    e_off = _bits(topo.mask(core, far(1, True)))
    e_loc = [e for e in _bits(topo.mask(core, sib)) if e not in e_off]
    n_land = {SIB: len(e_loc)}
    for o in FORWARD:
        n_land[_same(o)] = len(e_off)
        n_land[_other(o)] = len(e_loc)
    for o in DIRECT:
        n_land[_same(o)] = len(e_off)
        n_land[_other(o)] = len(e_off)

    sent = [0]

    def write(dst_core, dst_slot, src_slot, engines):
        rid, pid, _ = topo.addr(dst_core)
        sent[0] += len(engines)
        g.remote_dma_fused([RemoteDMATransfer(dst_ids=[DstId(rid=rid, pnc=pid)], dma_engine_mask=_mask(engines),
                                              remote_sem=sem["a%d" % dst_slot], src=slot(src_slot), dst=slot(dst_slot))],
                           local_sem=sem.sent)

    g.sync.dma_start(W[:, 0:128], T.w1[:, :]).then_inc(sem.wld, 16)
    g.scalar.dma_start(W[:, 128:256], T.w2[:, :]).then_inc(sem.wld, 16)
    g.sync.dma_start(X[:, :], T.x[:, :]).then_inc(sem.xld, 16)

    g.wait_ge(sem.wld, 32)
    write(far(FORWARD[0], True), _same(FORWARD[0]), OWN, e_off)
    write(sib, SIB, OWN, e_loc)
    for o in FORWARD[1:]:
        write(far(o, True), _same(o), OWN, e_off)
    for o in DIRECT:
        write(far(o, True), _same(o), OWN, e_off)
        write(far(o, False), _other(o), OWN, e_off)
    for o in FORWARD:
        g.wait_ge(sem["a%d" % _same(o)], n_land[_same(o)])
        write(sib, _other(o), _same(o), e_loc)

    pe = g.tensor
    n = len(UNITS)
    tile_of = [min(u, N_SLICES - 1) for u in range(n)]
    last_of = {0: max(u for u in range(n) if UNITS[u][1] < HALF), 1: max(u for u in range(n) if UNITS[u][2] > HALF)}
    n_y = {0: 0, 1: 0}

    def first(u):
        s, c0, c1 = UNITS[u]
        if u == 0 or UNITS[u - 1][0] != s:
            if s == OWN:
                pe.wait_ge(sem.wld, 32)
                pe.wait_ge(sem.xld, 16)
            else:
                pe.wait_ge(sem["a%d" % s], n_land[s])
        pe.matmul(T["h%d" % (u % N_HB)][:, 0:c1 - c0], W[:, s * SW:s * SW + 128], X[:, c0:c1], True, True).then_inc(sem["hd%d" % u], 1)

    def second(u):
        s, c0, c1 = UNITS[u]
        pe.wait_ge(sem["gd%d" % u], 1)
        for hf in (0, 1):
            lo, hi = max(c0, hf * HALF), min(c1, (hf + 1) * HALF)
            if lo >= hi:
                continue
            base = tile_of[u] * TOK
            pe.matmul(T["y%d" % hf][:, 0:HALF], W[:, s * SW + 128:(s + 1) * SW], G[:, base + lo:base + hi],
                      u == 0, u == last_of[hf]).then_inc(sem["yd%d" % hf], 1)
            n_y[hf] += 1

    pend = 0
    for u in range(n):
        first(u)
        while pend < n and min(pend + LOOK[pend], n - 1) <= u:
            second(pend)
            pend += 1

    for u in range(n):
        s, c0, c1 = UNITS[u]
        base = tile_of[u] * TOK
        g.scalar.wait_ge(sem["hd%d" % u], 1)
        g.scalar.activation(G[:, base + c0:base + c1], T["h%d" % (u % N_HB)][:, 0:c1 - c0],
                            ActivationFunctionType.Gelu_apprx_tanh).then_inc(sem["gd%d" % u], 1)

    for hf, q in ((0, g.sync), (1, g.scalar)):
        g.vector.wait_ge(sem["yd%d" % hf], n_y[hf])
        g.vector.tensor_copy(T.Yo[:, hf * HALF:(hf + 1) * HALF], T["y%d" % hf][:, 0:HALF]).then_inc(sem["cp%d" % hf], 1)
        q.wait_ge(sem["cp%d" % hf], 1)
        q.dma_start(T.y[:, hf * HALF:(hf + 1) * HALF], T.Yo[:, hf * HALF:(hf + 1) * HALF]).then_inc(sem["st%d" % hf], 16)
        q.wait_ge(sem["st%d" % hf], 16)

    g.wait_ge(sem.sent, sent[0])
